import numpy as np
import ml_dtypes


def mxq(x, axis, fmt="e4m3"):
    dtype, down = {"e4m3": (ml_dtypes.float8_e4m3fn, 7), "e5m2": (ml_dtypes.float8_e5m2, 14)}[fmt]
    v = np.moveaxis(np.asarray(x, np.float32).astype(ml_dtypes.bfloat16).astype(np.float64), axis, -1)
    blocks = v.reshape(v.shape[:-1] + (-1, 32))
    amax = np.abs(blocks).max(-1, keepdims=True)
    byte = np.maximum(np.where(amax > 0, np.frexp(amax)[1] - 1 + 127, 0) - down, 1)
    scale = np.exp2(byte - 127.0)
    codes = (blocks / scale).astype(np.float32).astype(dtype).astype(np.float64)
    return np.moveaxis((codes * scale).reshape(v.shape), -1, axis)


WIDE = False


def mx_kscale(k):
    if not WIDE:
        return np.ones(k)
    levels = np.array([10, -10, 5, -5, 0])
    if k % 512:
        return np.exp2(np.random.permutation(np.resize(levels, k // 32))).repeat(32)
    a = np.empty((k // 512, 16))
    for p in range(k // 512):
        a[p, :8] = np.random.permutation(np.resize(levels, 8))
        for g in range(8):
            far = levels[np.abs(levels - a[p, g]) >= 10]
            a[p, g + 8] = far[np.random.randint(len(far))]
    return np.exp2(a.ravel()).repeat(32)


def f64(x):
    return np.asarray(x).astype(np.float64)


def striped(idx):
    return np.tile(idx.reshape(-1, 16).T, (8, 1)).astype(np.uint16)


def unstriped(offs):
    return offs[:16].T.reshape(-1).astype(np.int64)


def striped8(idx):
    return np.concatenate([x.reshape(-1, 16).T for x in idx]).astype(np.uint16)


def runs(offs, k):
    lists = np.stack([offs[16 * r : 16 * r + 16].T.reshape(-1) for r in range(8)]).astype(np.int64)
    return lists[np.arange(k) % 512 // 64]


def pack_weight(w):
    k, n = w.shape
    w = f64(np.asarray(w, np.float32).astype(ml_dtypes.bfloat16)).reshape(k // 32, 32, n)
    amax = np.abs(w).max(1)
    byte = np.clip(np.where(amax > 0, np.frexp(amax)[1] - 1 + 127 - 7, 1), 1, 254)
    scaled = (w * np.exp2(127.0 - byte)[:, None, :]).reshape(k, n).astype(np.float32)
    words = np.ascontiguousarray(scaled.reshape(k // 512, 128, 4, n).transpose(0, 1, 3, 2)).astype(ml_dtypes.float8_e4m3fn).view(np.uint8)
    return words, np.ascontiguousarray(byte.astype(np.uint8).reshape(k // 512, 16, n))


def unpack_weight(words, scales):
    g, p, n, _ = words.shape
    vals = np.ascontiguousarray(words).view(ml_dtypes.float8_e4m3fn).astype(np.float64) * np.repeat(np.exp2(scales.astype(np.float64) - 127.0), 8, axis=1)[..., None]
    return vals.transpose(0, 1, 3, 2).reshape(g * 512, n)


E2M1 = np.array([0.0, 0.5, 1.0, 1.5, 2.0, 3.0, 4.0, 6.0, -0.0, -0.5, -1.0, -1.5, -2.0, -3.0, -4.0, -6.0])


def pack_fp4(w):
    k, n = w.shape
    w = f64(np.asarray(w, np.float32).astype(ml_dtypes.bfloat16)).reshape(k // 32, 32, n)
    amax = np.abs(w).max(1)
    mant, ex = np.frexp(amax / 6.0)
    byte = np.clip(np.where(amax > 0, np.where(mant > 0.5, ex, ex - 1) + 127, 1), 1, 254)
    scaled = (w * np.exp2(127.0 - byte)[:, None, :]).reshape(k, n).astype(np.float32)
    c = np.ascontiguousarray(scaled.reshape(k // 512, 128, 4, n).transpose(0, 1, 3, 2)).astype(ml_dtypes.float4_e2m1fn).view(np.uint8) & 0xF
    words = (c[..., 0::2] | (c[..., 1::2] << 4)).reshape(k // 512, 128, 2 * n)
    return np.ascontiguousarray(words), np.ascontiguousarray(byte.astype(np.uint8).reshape(k // 512, 16, n))


def unpack_fp4(words, scales):
    g, _, n = scales.shape
    words = np.ascontiguousarray(words).reshape(g, 128, n, 2)
    nib = np.empty((g, 128, n, 4), np.uint8)
    nib[..., 0::2] = words & 0xF
    nib[..., 1::2] = words >> 4
    vals = E2M1[nib] * np.repeat(np.exp2(scales.astype(np.float64) - 127.0), 8, axis=1)[..., None]
    return vals.transpose(0, 1, 3, 2).reshape(g * 512, n)


def sigmoid(v):
    return 1.0 / (1.0 + np.exp(-np.maximum(v, -700.0)))

def planes(y):
    n, m = y.shape
    v = y.astype(np.float32).astype(ml_dtypes.bfloat16).astype(np.float64).reshape(n // 32, 32, m)
    top = np.abs(v).max(1)
    byte = np.clip(np.where(top > 0, np.frexp(top)[1] - 1 + 127 - 7, 1), 1, 254)
    codes = (v * np.exp2(127.0 - byte)[:, None, :]).reshape(n, m).astype(np.float32).astype(ml_dtypes.float8_e4m3fn).view(np.uint8)
    words = codes.reshape(n // 512, 128, 4, m).transpose(0, 1, 3, 2)
    return np.ascontiguousarray(words), np.ascontiguousarray(byte.astype(np.uint8).reshape(n // 512, 16, m))


K, T, S, H, C, W = 512, 2048, 512, 512, 512, 2048


def setup_inputs():
    n = np.random.standard_normal
    s = mx_kscale(K)[:, None]
    packed_xT = pack_weight(n((K, T)) * s)
    packed_w1 = pack_fp4(n((K, H)) / np.sqrt(K) / s)
    return {
        "x_words": packed_xT[0],
        "x_scales": packed_xT[1],
        "w1_words": packed_w1[0],
        "w1_scales": packed_w1[1],
        "sl": np.random.uniform(1.0, 2.0, (H, 1)).astype(np.float32),
        "th": (0.5 * n((H, 1))).astype(np.float32),
        "gs": (np.random.uniform(0.5, 1.5, (K, 1)) / s).astype(np.float32),
        "offs": striped(np.random.permutation(T)[:S]),
        "n1": striped8(np.stack([np.random.permutation(S) for _ in range(8)])),
        "n2": striped8(np.stack([np.random.permutation(S) for _ in range(8)])),
        "cand": striped(np.random.permutation(T)[:C]),
        "n3": striped(np.random.randint(0, S, W)),
    }


def reference(x_words, x_scales, w1_words, w1_scales, sl, th, gs, offs, n1, n2, cand, n3):
    x_cand = unpack_weight(x_words, x_scales)[:, unstriped(cand)]
    xq = unpack_weight(x_words, x_scales)[:, unstriped(offs)]
    y = unpack_fp4(w1_words, w1_scales).T @ xq
    st = y - (y[np.arange(H)[:, None], runs(n1, H)])
    sg = sigmoid(f64(sl) * (st[np.arange(H)[:, None], runs(n2, H)] - f64(th)))
    z = f64(gs) * (y * sg)
    s = 0.0625 * ((x_cand.T @ mxq(z, 0, "e4m3")))
    mb = s[:, unstriped(n3)]
    sq = (mb) ** 2
    qs = sq.reshape(C, S, 4).sum(axis=2)
    out_0 = s / np.sqrt(qs + 0.5)
    return (out_0,) + planes(out_0)

@@ -1,0 +1,303 @@
+from contextlib import ExitStack
+
+import concourse.mybir as mybir
+
+K, T, S, H, C, W = 512, 2048, 512, 512, 512, 2048
+FLOPS = 2 * K * H * S + 2 * H * C * S
+
+F32 = mybir.dt.float32
+BF16 = mybir.dt.bfloat16
+I32 = mybir.dt.int32
+U32 = mybir.dt.uint32
+U16 = mybir.dt.uint16
+U8 = mybir.dt.uint8
+FP8X4 = mybir.dt.float8_e4m3fn_x4
+FP4X4 = mybir.dt.float4_e2m1fn_x4
+ACT = mybir.ActivationFunctionType
+ALU = mybir.AluOpType
+
+P = 128
+PACK = 4
+HALF = S // 2
+MEMBERS = W // S
+PIECE = 256
+FIRST_LOAD = 768
+CHUNKS = ((0, 256), (256, 128), (384, 128))
+GROUPS = ((0, 256), (256, 128), (384, 128))
+VECTOR_FIRST, VECTOR_EVERY, VECTOR_LAST = 3, 4, 28
+RING = 2
+
+
+def tile_picked_candehqgvar_none_po_kernel(tc, x_words, x_scales, w1_words, w1_scales, sl, th, gs, offs, n1, n2, cand, n3, out_0, out_1, out_2):
+    nc = tc.nc
+    with ExitStack() as ctx:
+        keep = ctx.enter_context(tc.tile_pool(name="keep", bufs=1))
+        ring = ctx.enter_context(tc.tile_pool(name="ring", bufs=RING))
+        psum = ctx.enter_context(tc.psum_pool(name="psum", bufs=1))
+
+        def sbuf(name, shape, dtype):
+            return keep.tile(shape, dtype, name=name, align_bytes=64)
+
+        def load_list(name, src):
+            tile = sbuf(name, list(src.shape), U16)
+            nc.sync.dma_start(tile[:], src)
+            return tile
+
+        def load_column(name, src):
+            tile = sbuf(name, [P, PACK], F32)
+            nc.sync.dma_start(tile[:], src.rearrange("(p t) o -> p (t o)", t=PACK))
+            return tile
+
+        x_scale_table = sbuf("x_scale_table", [P, T], U8)
+        w_scale_raw = keep.tile([P, H], U8, name="w_scale_raw", tag="w_scale_raw", align_bytes=64)
+
+        nc.vector.memset(x_scale_table[:].bitcast(I32), 0)
+        offs_t = load_list("offs_t", offs)
+        x_word_table = sbuf("x_word_table", [P, T], I32)
+        x_word_rows = x_words[0].rearrange("p n t -> p (n t)").bitcast(I32)
+        nc.sync.dma_start(x_word_table[:, :FIRST_LOAD], x_word_rows[:, :FIRST_LOAD])
+        for i in range(4):
+            nc.sync.dma_start(x_scale_table[i:P:32, :].bitcast(I32), x_scales[0][i:16:4, :].bitcast(I32))
+        nc.sync.dma_start(x_word_table[:, FIRST_LOAD:], x_word_rows[:, FIRST_LOAD:])
+        w_word_raw = sbuf("w_word_raw", [P, 2 * H], U8)
+        nc.sync.dma_start(w_word_raw[:].bitcast(I32), w1_words[0].bitcast(I32))
+        for q in range(4):
+            rows = w1_scales[0][4 * q : 4 * q + 4, :].bitcast(I32)
+            nc.sync.dma_start(
+                w_scale_raw[32 * q : 32 * q + 32, :].bitcast(I32), rows.unsqueeze(0).broadcast_to([8, 4, H // 4])
+            )
+        cand_t = load_list("cand_t", cand)
+        n1_t = load_list("n1_t", n1)
+        sl_t = load_column("sl_t", sl)
+        th_t = load_column("th_t", th)
+        n2_t = load_list("n2_t", n2)
+        gs_t = load_column("gs_t", gs)
+        n3_t = load_list("n3_t", n3)
+
+        w_words = sbuf("w_words", [P, 2 * H], U8)
+        w_scales = sbuf("w_scales", [P, H], U8)
+        nc.scalar.copy(
+            w_words[:].bitcast(U16).rearrange("p (t m) -> p t m", t=PACK),
+            w_word_raw[:].bitcast(U16).rearrange("p (m t) -> p t m", t=PACK),
+        )
+
+        tok_scales = sbuf("tok_scales", [P, S], U8)
+        nc.vector.tensor_copy(tok_scales[:], x_scale_table[:].indirect(offs_t[:]))
+        tok_words = [sbuf(f"tok_words{h}", [P, HALF], U32) for h in range(2)]
+        for h in range(2):
+            nc.vector.tensor_copy(tok_words[h][:], x_word_table[:].bitcast(U32).indirect(offs_t[:, 16 * h : 16 * h + 16]))
+            if h == 0:
+                nc.vector.tensor_copy(
+                    w_scales[:].rearrange("p (t m) -> p t m", t=PACK),
+                    w_scale_raw[:].rearrange("p (m t) -> p t m", t=PACK),
+                )
+
+
+        cand_words = keep.tile([P, C], U32, name="cand_words", tag="w_scale_raw", align_bytes=64)
+        nc.vector.tensor_copy(
+            cand_words[:].rearrange("p (t m) -> p m t", t=PACK), x_word_table[:].bitcast(U32).indirect(cand_t[:])
+        )
+
+        cand_scales = sbuf("cand_scales", [P, C], U8)
+        nc.vector.tensor_copy(cand_scales[:].rearrange("p (t m) -> p m t", t=PACK), x_scale_table[:].indirect(cand_t[:]))
+
+        gate_bias = sbuf("gate_bias", [P, PACK], F32)
+        nc.vector.scalar_tensor_tensor(gate_bias[:], sl_t[:], -1.0, th_t[:], ALU.mult, ALU.mult)
+
+        def cols(h):
+            return slice(h * HALF, (h + 1) * HALF)
+
+        def list_cols(h):
+            return slice(h * HALF // 16, (h + 1) * HALF // 16)
+
+        y_bank = {}
+        for t in range(PACK):
+            for h in range(2):
+                y_bank[t, h] = psum.tile([P, HALF], F32, name=f"y_bank{t}{h}", tag=f"bank{t}{h}")
+                nc.tensor.matmul_mx(
+                    out=y_bank[t, h][:],
+                    lhsT=w_words[:, 2 * P * t : 2 * P * (t + 1)].bitcast(FP4X4),
+                    lhsT_scale=w_scales[:, P * t : P * (t + 1)],
+                    rhs=tok_words[h][:].bitcast(FP8X4),
+                    rhs_scale=tok_scales[:, cols(h)],
+                    start=True,
+                    stop=True,
+                )
+
+        minus_y = [sbuf(f"minus_y{t}", [P, S], F32) for t in range(PACK)]
+        plus_y = [sbuf(f"plus_y{t}", [P, S], F32) for t in range(PACK)]
+        st = [sbuf(f"st{t}", [P, S], F32) for t in range(PACK)]
+        sg = [sbuf(f"sg{t}", [P, S], F32) for t in range(PACK)]
+        z_rows = [sbuf(f"z_rows{g}", [P, PACK, width], BF16) for g, (j0, width) in enumerate(GROUPS)]
+        z_words = [sbuf(f"z_words{g}", [P, width], U32) for g, (j0, width) in enumerate(GROUPS)]
+        z_scales = [sbuf(f"z_scales{g}", [P, width], U8) for g, (j0, width) in enumerate(GROUPS)]
+        sq = [sbuf(f"sq{t}", [P, S], F32) for t in range(PACK)]
+        s_bank = {}
+
+        def leave_psum(t):
+            for h in range(2):
+                nc.scalar.activation(minus_y[t][:, cols(h)], y_bank[t, h][:], ACT.Copy, scale=-1.0)
+                nc.scalar.activation(plus_y[t][:, cols(h)], y_bank[t, h][:], ACT.Copy)
+
+        def difference(t):
+            for h in range(2):
+                nc.vector.tensor_tensor(
+                    st[t][:, cols(h)], minus_y[t][:].indirect(n1_t[:, list_cols(h)]), plus_y[t][:, cols(h)], ALU.add
+                )
+
+        def gate(t, g):
+            j0, width = GROUPS[g]
+            nc.scalar.activation(
+                sg[t][:, j0 : j0 + width],
+                st[t][:].indirect(n2_t[:, j0 // 16 : (j0 + width) // 16]),
+                ACT.Sigmoid,
+                bias=gate_bias[:, t : t + 1],
+                scale=sl_t[:, t : t + 1],
+            )
+
+        def weigh(t, g):
+            j0, width = GROUPS[g]
+            nc.vector.scalar_tensor_tensor(
+                z_rows[g][:, t, :],
+                y_bank[t, j0 // HALF][:, j0 % HALF : j0 % HALF + width],
+                gs_t[:, t : t + 1],
+                sg[t][:, j0 : j0 + width],
+                ALU.mult,
+                ALU.mult,
+            )
+
+        def interleave(packed, rows):
+            nc.vector.tensor_copy(
+                packed.rearrange("p (c i) t -> p c t i", i=4), rows.rearrange("p t (c i) -> p c t i", i=4)
+            )
+
+        def quantise(g):
+            width = GROUPS[g][1]
+            z_packed = keep.tile([P, width, PACK], BF16, name=f"z_packed{g}", tag="z_packed", align_bytes=64)
+            interleave(z_packed[:], z_rows[g][:])
+            nc.vector.quantize_mx(
+                out=z_words[g][:].bitcast(FP8X4), scales=z_scales[g][:], in_=z_packed[:].rearrange("p c t -> p (c t)")
+            )
+
+        def score(g):
+            j0, width = GROUPS[g]
+            h = j0 // HALF
+            for t in range(PACK):
+                if (t, h) not in s_bank:
+                    s_bank[t, h] = psum.tile([P, HALF], F32, name=f"s_bank{t}{h}", tag=f"bank{t}{h}")
+                nc.tensor.matmul_mx(
+                    out=s_bank[t, h][:, j0 % HALF : j0 % HALF + width],
+                    lhsT=cand_words[:, P * t : P * (t + 1)].bitcast(FP8X4),
+                    lhsT_scale=cand_scales[:, P * t : P * (t + 1)],
+                    rhs=z_words[g][:].bitcast(FP8X4),
+                    rhs_scale=z_scales[g][:],
+                    start=True,
+                    stop=True,
+                )
+                if (j0 + width) % HALF == 0:
+                    nc.scalar.activation(sq[t][:, cols(h)], s_bank[t, h][:], ACT.Square, scale=0.0625)
+
+        leave_psum(0)
+        for t in range(PACK):
+            if t + 1 < PACK:
+                leave_psum(t + 1)
+            difference(t)
+        for g in range(len(GROUPS)):
+            for t in range(PACK):
+                gate(t, g)
+        for g in range(len(GROUPS)):
+            for t in range(PACK):
+                weigh(t, g)
+            quantise(g)
+            if g == 0:
+                score(g)
+        for g in range(1, len(GROUPS)):
+            score(g)
+
+        out_words = sbuf("out_words", [P, S], U32)
+        out_scales = sbuf("out_scales", [P, S], U8)
+        out_rows = out_0.rearrange("(p t) j -> p t j", t=PACK)
+        out_word_rows = out_1[0].rearrange("p n t -> p (n t)").bitcast(I32)
+
+        units = [(c, t) for c in range(len(CHUNKS)) for t in range(PACK)]
+        result = [sbuf(f"result{c}", [P, PACK, width], F32) for c, (j0, width) in enumerate(CHUNKS)]
+        members, pairs, qs, inv_root = {}, {}, {}, {}
+
+        def fetch(u, on_vector):
+            c, t = units[u]
+            j0, width = CHUNKS[c]
+            if u not in members:
+                members[u] = ring.tile([P, width * MEMBERS], F32, name=f"members{u}", tag="members")
+            for k in range(width * MEMBERS // PIECE):
+                col = (j0 * MEMBERS + k * PIECE) // 16
+                looked_up = sq[t][:].indirect(n3_t[:, col : col + PIECE // 16])
+                dst = members[u][:, k * PIECE : (k + 1) * PIECE]
+                q = (j0 * PACK + t * width) * MEMBERS // PIECE + k
+                if q < VECTOR_FIRST or (q % VECTOR_EVERY == 0 and q <= VECTOR_LAST):
+                    if on_vector:
+                        nc.vector.tensor_copy(dst, looked_up)
+                elif not on_vector:
+                    nc.scalar.activation(dst, looked_up, ACT.Copy)
+
+        def add_pairs(u):
+            width = CHUNKS[units[u][0]][1]
+            quads = members[u][:].rearrange("p (j m) -> p j m", m=MEMBERS)
+            pairs[u] = sbuf(f"pairs{u}", [P, width, 2], F32)
+            nc.vector.tensor_tensor(pairs[u][:], quads[:, :, 0:2], quads[:, :, 2:4], ALU.add)
+
+        def root(u):
+            width = CHUNKS[units[u][0]][1]
+            qs[u] = sbuf(f"qs{u}", [P, width], F32)
+            nc.vector.tensor_tensor(qs[u][:], pairs[u][:, :, 0], pairs[u][:, :, 1], ALU.add)
+            inv_root[u] = sbuf(f"inv_root{u}", [P, width], F32)
+            nc.scalar.activation(inv_root[u][:], qs[u][:], ACT.Abs_reciprocal_sqrt, bias=0.5)
+
+        def finish(u):
+            c, t = units[u]
+            j0, width = CHUNKS[c]
+            h = j0 // HALF
+            js = slice(j0, j0 + width)
+            bank_js = slice(j0 - h * HALF, j0 - h * HALF + width)
+            nc.vector.scalar_tensor_tensor(
+                result[c][:, t, :], s_bank[t, h][:, bank_js], 0.0625, inv_root[u][:], ALU.mult, ALU.mult
+            )
+            nc.sync.dma_start(out_rows[:, t, js], result[c][:, t, :])
+
+        def pack(c):
+            j0, width = CHUNKS[c]
+            packed[c] = sbuf(f"out_packed{c}", [P, width, PACK], BF16)
+            interleave(packed[c][:], result[c][:])
+
+        def hand_on(c):
+            j0, width = CHUNKS[c]
+            js = slice(j0, j0 + width)
+            nc.vector.quantize_mx(
+                out=out_words[:, js].bitcast(FP8X4),
+                scales=out_scales[:, js],
+                in_=packed[c][:].rearrange("p c t -> p (c t)"),
+            )
+            nc.sync.dma_start(out_word_rows[:, js], out_words[:, js].bitcast(I32))
+
+        packed = {}
+        n_units = len(units)
+        fetch(0, True)
+        fetch(0, False)
+        fetch(1, False)
+        for u in range(1, n_units + 3):
+            if u - 1 < n_units:
+                add_pairs(u - 1)
+            if u < n_units:
+                fetch(u, True)
+            if 0 <= u - 3 and units[u - 3][1] == PACK - 1:
+                hand_on(units[u - 3][0])
+            if u - 1 < n_units:
+                root(u - 1)
+            if u + 1 < n_units:
+                fetch(u + 1, False)
+            if 0 <= u - 2 < n_units:
+                finish(u - 2)
+                if units[u - 2][1] == PACK - 1:
+                    pack(units[u - 2][0])
+        for i in range(4):
+            queue = nc.sync if i < 2 else nc.scalar
+            queue.dma_start(out_2[0][i:16:4, :].bitcast(I32), out_scales[i:P:32, :].bitcast(I32))

@@ -52,6 +52,10 @@ def tile_picked_candehqgvar_none_po_kernel(tc, x_words, x_scales, w1_words, w1_s
         w_scale_raw = keep.tile([P, H], U8, name="w_scale_raw", tag="w_scale_raw", align_bytes=64)
 
         nc.vector.memset(x_scale_table[:].bitcast(I32), 0)
+        warm_in = sbuf("warm_in", [P, 1], F32)
+        warm_out = sbuf("warm_out", [P, 2], F32)
+        nc.gpsimd.memset(warm_in[:], 0.0)
+        nc.scalar.activation(warm_out[:, 0:1], warm_in[:], ACT.Sigmoid)
         offs_t = load_list("offs_t", offs)
         x_word_table = sbuf("x_word_table", [P, T], I32)
         x_word_rows = x_words[0].rearrange("p n t -> p (n t)").bitcast(I32)
@@ -205,6 +209,7 @@ def tile_picked_candehqgvar_none_po_kernel(tc, x_words, x_scales, w1_words, w1_s
         for g in range(len(GROUPS)):
             for t in range(PACK):
                 gate(t, g)
+        nc.scalar.activation(warm_out[:, 1:2], sg[PACK - 1][:, S - 1 : S], ACT.Abs_reciprocal_sqrt, bias=0.5)
         for g in range(len(GROUPS)):
             for t in range(PACK):
                 weigh(t, g)

@@ -24,8 +24,11 @@ PIECE = 256
 FIRST_LOAD = 768
 CHUNKS = ((0, 256), (256, 128), (384, 128))
 GROUPS = ((0, 256), (256, 128), (384, 128))
-VECTOR_FIRST, VECTOR_EVERY, VECTOR_LAST = 3, 4, 28
-RING = 2
+VECTOR_FIRST, VECTOR_EVERY, VECTOR_LAST = 4, 3, 27
+RING = 4
+GPSIMD_UNITS = (0, 1, 3, 4, 6, 7)
+REDUCE_UNITS = (2, 5)
+LAG = 2
 
 
 def tile_picked_candehqgvar_none_po_kernel(tc, x_words, x_scales, w1_words, w1_scales, sl, th, gs, offs, n1, n2, cand, n3, out_0, out_1, out_2):
@@ -90,12 +93,12 @@ def tile_picked_candehqgvar_none_po_kernel(tc, x_words, x_scales, w1_words, w1_s
         tok_words = [sbuf(f"tok_words{h}", [P, HALF], U32) for h in range(2)]
         for h in range(2):
             nc.vector.tensor_copy(tok_words[h][:], x_word_table[:].bitcast(U32).indirect(offs_t[:, 16 * h : 16 * h + 16]))
-            if h == 0:
-                nc.vector.tensor_copy(
-                    w_scales[:].rearrange("p (t m) -> p t m", t=PACK),
-                    w_scale_raw[:].rearrange("p (m t) -> p t m", t=PACK),
-                )
 
+
+        w_scales_dealt = w_scales[:].rearrange("p (t m) -> p t m", t=PACK)
+        w_scales_given = w_scale_raw[:].rearrange("p (m t) -> p t m", t=PACK)
+        nc.vector.tensor_copy(w_scales_dealt[:, 0, :], w_scales_given[:, 0, :])
+        nc.vector.tensor_copy(w_scales_dealt[:, 1:, :], w_scales_given[:, 1:, :])
 
         cand_words = keep.tile([P, C], U32, name="cand_words", tag="w_scale_raw", align_bytes=64)
         nc.vector.tensor_copy(
@@ -244,16 +247,28 @@ def tile_picked_candehqgvar_none_po_kernel(tc, x_words, x_scales, w1_words, w1_s
                 elif not on_vector:
                     nc.scalar.activation(dst, looked_up, ACT.Copy)
 
+        def adder(u):
+            return nc.gpsimd if u in GPSIMD_UNITS else nc.vector
+
         def add_pairs(u):
             width = CHUNKS[units[u][0]][1]
+            if u in REDUCE_UNITS:
+                return
             quads = members[u][:].rearrange("p (j m) -> p j m", m=MEMBERS)
             pairs[u] = sbuf(f"pairs{u}", [P, width, 2], F32)
-            nc.vector.tensor_tensor(pairs[u][:], quads[:, :, 0:2], quads[:, :, 2:4], ALU.add)
+            if u in GPSIMD_UNITS:
+                halves = members[u][:].rearrange("p (j m) -> p j m", m=2)
+                nc.gpsimd.tensor_tensor(pairs[u][:].rearrange("p j m -> p (j m)"), halves[:, :, 0], halves[:, :, 1], ALU.add)
+            else:
+                nc.vector.tensor_tensor(pairs[u][:], quads[:, :, 0:2], quads[:, :, 2:4], ALU.add)
 
         def root(u):
             width = CHUNKS[units[u][0]][1]
             qs[u] = sbuf(f"qs{u}", [P, width], F32)
-            nc.vector.tensor_tensor(qs[u][:], pairs[u][:, :, 0], pairs[u][:, :, 1], ALU.add)
+            if u in REDUCE_UNITS:
+                nc.vector.tensor_reduce(qs[u][:], members[u][:].rearrange("p (j m) -> p j m", m=MEMBERS), mybir.AxisListType.X, ALU.add)
+            else:
+                adder(u).tensor_tensor(qs[u][:], pairs[u][:, :, 0], pairs[u][:, :, 1], ALU.add)
             inv_root[u] = sbuf(f"inv_root{u}", [P, width], F32)
             nc.scalar.activation(inv_root[u][:], qs[u][:], ACT.Abs_reciprocal_sqrt, bias=0.5)
 
@@ -288,21 +303,21 @@ def tile_picked_candehqgvar_none_po_kernel(tc, x_words, x_scales, w1_words, w1_s
         fetch(0, True)
         fetch(0, False)
         fetch(1, False)
-        for u in range(1, n_units + 3):
+        for u in range(1, n_units + LAG + 1):
             if u - 1 < n_units:
                 add_pairs(u - 1)
             if u < n_units:
                 fetch(u, True)
-            if 0 <= u - 3 and units[u - 3][1] == PACK - 1:
-                hand_on(units[u - 3][0])
+            if 0 <= u - LAG - 1 and units[u - LAG - 1][1] == PACK - 1:
+                hand_on(units[u - LAG - 1][0])
             if u - 1 < n_units:
                 root(u - 1)
             if u + 1 < n_units:
                 fetch(u + 1, False)
-            if 0 <= u - 2 < n_units:
-                finish(u - 2)
-                if units[u - 2][1] == PACK - 1:
-                    pack(units[u - 2][0])
+            if 0 <= u - LAG < n_units:
+                finish(u - LAG)
+                if units[u - LAG][1] == PACK - 1:
+                    pack(units[u - LAG][0])
         for i in range(4):
             queue = nc.sync if i < 2 else nc.scalar
             queue.dma_start(out_2[0][i:16:4, :].bitcast(I32), out_scales[i:P:32, :].bitcast(I32))

@@ -18,20 +18,23 @@ ALU = mybir.AluOpType
 
 P = 128
 PACK = 4
+QUADRANT = 32
+SCALE_ROWS = 4
+BLOCKS = 16
+PER_COLUMN = 16
 HALF = S // 2
 MEMBERS = W // S
 PIECE = 256
 FIRST_LOAD = 768
-CHUNKS = ((0, 256), (256, 128), (384, 128))
-GROUPS = ((0, 256), (256, 128), (384, 128))
-VECTOR_FIRST, VECTOR_EVERY, VECTOR_LAST = 4, 3, 27
-RING = 4
-GPSIMD_UNITS = (0, 1, 3, 4, 6, 7)
-REDUCE_UNITS = (2, 5)
-LAG = 2
+RANGES = ((0, 256), (256, 128), (384, 128))
+VECTOR_FIRST, VECTOR_EVERY, VECTOR_LAST = 4, 4, 26
+RING = 3
+LAG = 3
 
 
-def tile_picked_candehqgvar_none_po_kernel(tc, x_words, x_scales, w1_words, w1_scales, sl, th, gs, offs, n1, n2, cand, n3, out_0, out_1, out_2):
+def tile_picked_candehqgvar_none_po_kernel(
+    tc, x_words, x_scales, w1_words, w1_scales, sl, th, gs, offs, n1, n2, cand, n3, out_0, out_1, out_2
+):
     nc = tc.nc
     with ExitStack() as ctx:
         keep = ctx.enter_context(tc.tile_pool(name="keep", bufs=1))
@@ -46,10 +49,19 @@ def tile_picked_candehqgvar_none_po_kernel(tc, x_words, x_scales, w1_words, w1_s
             nc.sync.dma_start(tile[:], src)
             return tile
 
-        def load_column(name, src):
+        def load_per_row(name, src):
             tile = sbuf(name, [P, PACK], F32)
             nc.sync.dma_start(tile[:], src.rearrange("(p t) o -> p (t o)", t=PACK))
             return tile
+
+        def half_cols(h):
+            return slice(h * HALF, (h + 1) * HALF)
+
+        def list_cols(first, count):
+            return slice(first // PER_COLUMN, (first + count) // PER_COLUMN)
+
+        def in_bank(banks, t, j0, width):
+            return banks[t, j0 // HALF][:, j0 % HALF : j0 % HALF + width]
 
         x_scale_table = sbuf("x_scale_table", [P, T], U8)
         w_scale_raw = keep.tile([P, H], U8, name="w_scale_raw", tag="w_scale_raw", align_bytes=64)
@@ -59,26 +71,30 @@ def tile_picked_candehqgvar_none_po_kernel(tc, x_words, x_scales, w1_words, w1_s
         warm_out = sbuf("warm_out", [P, 2], F32)
         nc.gpsimd.memset(warm_in[:], 0.0)
         nc.scalar.activation(warm_out[:, 0:1], warm_in[:], ACT.Sigmoid)
+
         offs_t = load_list("offs_t", offs)
         x_word_table = sbuf("x_word_table", [P, T], I32)
         x_word_rows = x_words[0].rearrange("p n t -> p (n t)").bitcast(I32)
         nc.sync.dma_start(x_word_table[:, :FIRST_LOAD], x_word_rows[:, :FIRST_LOAD])
-        for i in range(4):
-            nc.sync.dma_start(x_scale_table[i:P:32, :].bitcast(I32), x_scales[0][i:16:4, :].bitcast(I32))
+        for i in range(SCALE_ROWS):
+            nc.sync.dma_start(
+                x_scale_table[i:P:QUADRANT, :].bitcast(I32), x_scales[0][i:BLOCKS:SCALE_ROWS, :].bitcast(I32)
+            )
         nc.sync.dma_start(x_word_table[:, FIRST_LOAD:], x_word_rows[:, FIRST_LOAD:])
         w_word_raw = sbuf("w_word_raw", [P, 2 * H], U8)
         nc.sync.dma_start(w_word_raw[:].bitcast(I32), w1_words[0].bitcast(I32))
-        for q in range(4):
-            rows = w1_scales[0][4 * q : 4 * q + 4, :].bitcast(I32)
+        for q in range(P // QUADRANT):
+            rows = w1_scales[0][SCALE_ROWS * q : SCALE_ROWS * (q + 1), :].bitcast(I32)
             nc.sync.dma_start(
-                w_scale_raw[32 * q : 32 * q + 32, :].bitcast(I32), rows.unsqueeze(0).broadcast_to([8, 4, H // 4])
+                w_scale_raw[QUADRANT * q : QUADRANT * (q + 1), :].bitcast(I32),
+                rows.unsqueeze(0).broadcast_to([QUADRANT // SCALE_ROWS, SCALE_ROWS, rows.shape[1]]),
             )
         cand_t = load_list("cand_t", cand)
         n1_t = load_list("n1_t", n1)
-        sl_t = load_column("sl_t", sl)
-        th_t = load_column("th_t", th)
+        sl_t = load_per_row("sl_t", sl)
+        th_t = load_per_row("th_t", th)
         n2_t = load_list("n2_t", n2)
-        gs_t = load_column("gs_t", gs)
+        gs_t = load_per_row("gs_t", gs)
         n3_t = load_list("n3_t", n3)
 
         w_words = sbuf("w_words", [P, 2 * H], U8)
@@ -92,8 +108,9 @@ def tile_picked_candehqgvar_none_po_kernel(tc, x_words, x_scales, w1_words, w1_s
         nc.vector.tensor_copy(tok_scales[:], x_scale_table[:].indirect(offs_t[:]))
         tok_words = [sbuf(f"tok_words{h}", [P, HALF], U32) for h in range(2)]
         for h in range(2):
-            nc.vector.tensor_copy(tok_words[h][:], x_word_table[:].bitcast(U32).indirect(offs_t[:, 16 * h : 16 * h + 16]))
-
+            nc.vector.tensor_copy(
+                tok_words[h][:], x_word_table[:].bitcast(U32).indirect(offs_t[:, list_cols(h * HALF, HALF)])
+            )
 
         w_scales_dealt = w_scales[:].rearrange("p (t m) -> p t m", t=PACK)
         w_scales_given = w_scale_raw[:].rearrange("p (m t) -> p t m", t=PACK)
@@ -104,18 +121,13 @@ def tile_picked_candehqgvar_none_po_kernel(tc, x_words, x_scales, w1_words, w1_s
         nc.vector.tensor_copy(
             cand_words[:].rearrange("p (t m) -> p m t", t=PACK), x_word_table[:].bitcast(U32).indirect(cand_t[:])
         )
-
         cand_scales = sbuf("cand_scales", [P, C], U8)
-        nc.vector.tensor_copy(cand_scales[:].rearrange("p (t m) -> p m t", t=PACK), x_scale_table[:].indirect(cand_t[:]))
+        nc.vector.tensor_copy(
+            cand_scales[:].rearrange("p (t m) -> p m t", t=PACK), x_scale_table[:].indirect(cand_t[:])
+        )
 
         gate_bias = sbuf("gate_bias", [P, PACK], F32)
         nc.vector.scalar_tensor_tensor(gate_bias[:], sl_t[:], -1.0, th_t[:], ALU.mult, ALU.mult)
-
-        def cols(h):
-            return slice(h * HALF, (h + 1) * HALF)
-
-        def list_cols(h):
-            return slice(h * HALF // 16, (h + 1) * HALF // 16)
 
         y_bank = {}
         for t in range(PACK):
@@ -126,7 +138,7 @@ def tile_picked_candehqgvar_none_po_kernel(tc, x_words, x_scales, w1_words, w1_s
                     lhsT=w_words[:, 2 * P * t : 2 * P * (t + 1)].bitcast(FP4X4),
                     lhsT_scale=w_scales[:, P * t : P * (t + 1)],
                     rhs=tok_words[h][:].bitcast(FP8X4),
-                    rhs_scale=tok_scales[:, cols(h)],
+                    rhs_scale=tok_scales[:, half_cols(h)],
                     start=True,
                     stop=True,
                 )
@@ -135,38 +147,41 @@ def tile_picked_candehqgvar_none_po_kernel(tc, x_words, x_scales, w1_words, w1_s
         plus_y = [sbuf(f"plus_y{t}", [P, S], F32) for t in range(PACK)]
         st = [sbuf(f"st{t}", [P, S], F32) for t in range(PACK)]
         sg = [sbuf(f"sg{t}", [P, S], F32) for t in range(PACK)]
-        z_rows = [sbuf(f"z_rows{g}", [P, PACK, width], BF16) for g, (j0, width) in enumerate(GROUPS)]
-        z_words = [sbuf(f"z_words{g}", [P, width], U32) for g, (j0, width) in enumerate(GROUPS)]
-        z_scales = [sbuf(f"z_scales{g}", [P, width], U8) for g, (j0, width) in enumerate(GROUPS)]
+        z_rows = [sbuf(f"z_rows{r}", [P, PACK, width], BF16) for r, (j0, width) in enumerate(RANGES)]
+        z_words = [sbuf(f"z_words{r}", [P, width], U32) for r, (j0, width) in enumerate(RANGES)]
+        z_scales = [sbuf(f"z_scales{r}", [P, width], U8) for r, (j0, width) in enumerate(RANGES)]
         sq = [sbuf(f"sq{t}", [P, S], F32) for t in range(PACK)]
         s_bank = {}
 
         def leave_psum(t):
             for h in range(2):
-                nc.scalar.activation(minus_y[t][:, cols(h)], y_bank[t, h][:], ACT.Copy, scale=-1.0)
-                nc.scalar.activation(plus_y[t][:, cols(h)], y_bank[t, h][:], ACT.Copy)
+                nc.scalar.activation(minus_y[t][:, half_cols(h)], y_bank[t, h][:], ACT.Copy, scale=-1.0)
+                nc.scalar.activation(plus_y[t][:, half_cols(h)], y_bank[t, h][:], ACT.Copy)
 
         def difference(t):
             for h in range(2):
                 nc.vector.tensor_tensor(
-                    st[t][:, cols(h)], minus_y[t][:].indirect(n1_t[:, list_cols(h)]), plus_y[t][:, cols(h)], ALU.add
+                    st[t][:, half_cols(h)],
+                    minus_y[t][:].indirect(n1_t[:, list_cols(h * HALF, HALF)]),
+                    plus_y[t][:, half_cols(h)],
+                    ALU.add,
                 )
 
-        def gate(t, g):
-            j0, width = GROUPS[g]
+        def gate(t, r):
+            j0, width = RANGES[r]
             nc.scalar.activation(
                 sg[t][:, j0 : j0 + width],
-                st[t][:].indirect(n2_t[:, j0 // 16 : (j0 + width) // 16]),
+                st[t][:].indirect(n2_t[:, list_cols(j0, width)]),
                 ACT.Sigmoid,
                 bias=gate_bias[:, t : t + 1],
                 scale=sl_t[:, t : t + 1],
             )
 
-        def weigh(t, g):
-            j0, width = GROUPS[g]
+        def weigh(t, r):
+            j0, width = RANGES[r]
             nc.vector.scalar_tensor_tensor(
-                z_rows[g][:, t, :],
-                y_bank[t, j0 // HALF][:, j0 % HALF : j0 % HALF + width],
+                z_rows[r][:, t, :],
+                in_bank(y_bank, t, j0, width),
                 gs_t[:, t : t + 1],
                 sg[t][:, j0 : j0 + width],
                 ALU.mult,
@@ -178,146 +193,138 @@ def tile_picked_candehqgvar_none_po_kernel(tc, x_words, x_scales, w1_words, w1_s
                 packed.rearrange("p (c i) t -> p c t i", i=4), rows.rearrange("p t (c i) -> p c t i", i=4)
             )
 
-        def quantise(g):
-            width = GROUPS[g][1]
-            z_packed = keep.tile([P, width, PACK], BF16, name=f"z_packed{g}", tag="z_packed", align_bytes=64)
-            interleave(z_packed[:], z_rows[g][:])
+        def quantise_z(r):
+            z_packed = keep.tile([P, RANGES[r][1], PACK], BF16, name=f"z_packed{r}", tag="z_packed", align_bytes=64)
+            interleave(z_packed[:], z_rows[r][:])
             nc.vector.quantize_mx(
-                out=z_words[g][:].bitcast(FP8X4), scales=z_scales[g][:], in_=z_packed[:].rearrange("p c t -> p (c t)")
+                out=z_words[r][:].bitcast(FP8X4), scales=z_scales[r][:], in_=z_packed[:].rearrange("p c t -> p (c t)")
             )
 
-        def score(g):
-            j0, width = GROUPS[g]
+        def score(r):
+            j0, width = RANGES[r]
             h = j0 // HALF
             for t in range(PACK):
                 if (t, h) not in s_bank:
                     s_bank[t, h] = psum.tile([P, HALF], F32, name=f"s_bank{t}{h}", tag=f"bank{t}{h}")
                 nc.tensor.matmul_mx(
-                    out=s_bank[t, h][:, j0 % HALF : j0 % HALF + width],
+                    out=in_bank(s_bank, t, j0, width),
                     lhsT=cand_words[:, P * t : P * (t + 1)].bitcast(FP8X4),
                     lhsT_scale=cand_scales[:, P * t : P * (t + 1)],
-                    rhs=z_words[g][:].bitcast(FP8X4),
-                    rhs_scale=z_scales[g][:],
+                    rhs=z_words[r][:].bitcast(FP8X4),
+                    rhs_scale=z_scales[r][:],
                     start=True,
                     stop=True,
                 )
                 if (j0 + width) % HALF == 0:
-                    nc.scalar.activation(sq[t][:, cols(h)], s_bank[t, h][:], ACT.Square, scale=0.0625)
+                    nc.scalar.activation(sq[t][:, half_cols(h)], s_bank[t, h][:], ACT.Square, scale=0.0625)
 
         leave_psum(0)
         for t in range(PACK):
             if t + 1 < PACK:
                 leave_psum(t + 1)
             difference(t)
-        for g in range(len(GROUPS)):
+        for r in range(len(RANGES)):
             for t in range(PACK):
-                gate(t, g)
+                gate(t, r)
         nc.scalar.activation(warm_out[:, 1:2], sg[PACK - 1][:, S - 1 : S], ACT.Abs_reciprocal_sqrt, bias=0.5)
-        for g in range(len(GROUPS)):
+        for r in range(len(RANGES)):
             for t in range(PACK):
-                weigh(t, g)
-            quantise(g)
-            if g == 0:
-                score(g)
-        for g in range(1, len(GROUPS)):
-            score(g)
+                weigh(t, r)
+            quantise_z(r)
+            if r == 0:
+                score(r)
+        for r in range(1, len(RANGES)):
+            score(r)
 
         out_words = sbuf("out_words", [P, S], U32)
         out_scales = sbuf("out_scales", [P, S], U8)
         out_rows = out_0.rearrange("(p t) j -> p t j", t=PACK)
         out_word_rows = out_1[0].rearrange("p n t -> p (n t)").bitcast(I32)
 
-        units = [(c, t) for c in range(len(CHUNKS)) for t in range(PACK)]
-        result = [sbuf(f"result{c}", [P, PACK, width], F32) for c, (j0, width) in enumerate(CHUNKS)]
-        members, pairs, qs, inv_root = {}, {}, {}, {}
+        units = [(r, t) for r in range(len(RANGES)) for t in range(PACK)]
+        last_unit = len(units) - 1
+        result = [sbuf(f"result{r}", [P, PACK, width], F32) for r, (j0, width) in enumerate(RANGES)]
+        members, pairs, inv_root, out_packed = {}, {}, {}, {}
 
         def fetch(u, on_vector):
-            c, t = units[u]
-            j0, width = CHUNKS[c]
+            r, t = units[u]
+            j0, width = RANGES[r]
             if u not in members:
                 members[u] = ring.tile([P, width * MEMBERS], F32, name=f"members{u}", tag="members")
+            first_piece = (j0 * PACK + t * width) * MEMBERS // PIECE
             for k in range(width * MEMBERS // PIECE):
-                col = (j0 * MEMBERS + k * PIECE) // 16
-                looked_up = sq[t][:].indirect(n3_t[:, col : col + PIECE // 16])
+                looked_up = sq[t][:].indirect(n3_t[:, list_cols(j0 * MEMBERS + k * PIECE, PIECE)])
                 dst = members[u][:, k * PIECE : (k + 1) * PIECE]
-                q = (j0 * PACK + t * width) * MEMBERS // PIECE + k
-                if q < VECTOR_FIRST or (q % VECTOR_EVERY == 0 and q <= VECTOR_LAST):
-                    if on_vector:
-                        nc.vector.tensor_copy(dst, looked_up)
-                elif not on_vector:
+                piece = first_piece + k
+                for_vector = piece < VECTOR_FIRST or (piece % VECTOR_EVERY == 1 and piece <= VECTOR_LAST)
+                if for_vector and on_vector:
+                    nc.vector.tensor_copy(dst, looked_up)
+                if not for_vector and not on_vector:
                     nc.scalar.activation(dst, looked_up, ACT.Copy)
 
-        def adder(u):
-            return nc.gpsimd if u in GPSIMD_UNITS else nc.vector
+        def by_column(u):
+            return members[u][:].rearrange("p (j m) -> p j m", m=MEMBERS)
 
         def add_pairs(u):
-            width = CHUNKS[units[u][0]][1]
-            if u in REDUCE_UNITS:
-                return
-            quads = members[u][:].rearrange("p (j m) -> p j m", m=MEMBERS)
-            pairs[u] = sbuf(f"pairs{u}", [P, width, 2], F32)
-            if u in GPSIMD_UNITS:
-                halves = members[u][:].rearrange("p (j m) -> p j m", m=2)
-                nc.gpsimd.tensor_tensor(pairs[u][:].rearrange("p j m -> p (j m)"), halves[:, :, 0], halves[:, :, 1], ALU.add)
-            else:
-                nc.vector.tensor_tensor(pairs[u][:], quads[:, :, 0:2], quads[:, :, 2:4], ALU.add)
+            pairs[u] = sbuf(f"pairs{u}", [P, RANGES[units[u][0]][1], 2], F32)
+            nc.vector.tensor_tensor(pairs[u][:], by_column(u)[:, :, 0:2], by_column(u)[:, :, 2:4], ALU.add)
 
         def root(u):
-            width = CHUNKS[units[u][0]][1]
-            qs[u] = sbuf(f"qs{u}", [P, width], F32)
-            if u in REDUCE_UNITS:
-                nc.vector.tensor_reduce(qs[u][:], members[u][:].rearrange("p (j m) -> p j m", m=MEMBERS), mybir.AxisListType.X, ALU.add)
+            width = RANGES[units[u][0]][1]
+            qs = sbuf(f"qs{u}", [P, width], F32)
+            if u == last_unit:
+                nc.vector.tensor_reduce(qs[:], by_column(u), mybir.AxisListType.X, ALU.add)
             else:
-                adder(u).tensor_tensor(qs[u][:], pairs[u][:, :, 0], pairs[u][:, :, 1], ALU.add)
+                nc.vector.tensor_tensor(qs[:], pairs[u][:, :, 0], pairs[u][:, :, 1], ALU.add)
             inv_root[u] = sbuf(f"inv_root{u}", [P, width], F32)
-            nc.scalar.activation(inv_root[u][:], qs[u][:], ACT.Abs_reciprocal_sqrt, bias=0.5)
+            nc.scalar.activation(inv_root[u][:], qs[:], ACT.Abs_reciprocal_sqrt, bias=0.5)
 
         def finish(u):
-            c, t = units[u]
-            j0, width = CHUNKS[c]
-            h = j0 // HALF
-            js = slice(j0, j0 + width)
-            bank_js = slice(j0 - h * HALF, j0 - h * HALF + width)
+            r, t = units[u]
+            j0, width = RANGES[r]
             nc.vector.scalar_tensor_tensor(
-                result[c][:, t, :], s_bank[t, h][:, bank_js], 0.0625, inv_root[u][:], ALU.mult, ALU.mult
+                result[r][:, t, :], in_bank(s_bank, t, j0, width), 0.0625, inv_root[u][:], ALU.mult, ALU.mult
             )
-            nc.sync.dma_start(out_rows[:, t, js], result[c][:, t, :])
+            nc.sync.dma_start(out_rows[:, t, j0 : j0 + width], result[r][:, t, :])
 
-        def pack(c):
-            j0, width = CHUNKS[c]
-            packed[c] = sbuf(f"out_packed{c}", [P, width, PACK], BF16)
-            interleave(packed[c][:], result[c][:])
+        def pack(r):
+            out_packed[r] = sbuf(f"out_packed{r}", [P, RANGES[r][1], PACK], BF16)
+            interleave(out_packed[r][:], result[r][:])
 
-        def hand_on(c):
-            j0, width = CHUNKS[c]
+        def hand_on(r):
+            j0, width = RANGES[r]
             js = slice(j0, j0 + width)
             nc.vector.quantize_mx(
                 out=out_words[:, js].bitcast(FP8X4),
                 scales=out_scales[:, js],
-                in_=packed[c][:].rearrange("p c t -> p (c t)"),
+                in_=out_packed[r][:].rearrange("p c t -> p (c t)"),
             )
             nc.sync.dma_start(out_word_rows[:, js], out_words[:, js].bitcast(I32))
 
-        packed = {}
-        n_units = len(units)
+        def closes_range(u):
+            return 0 <= u <= last_unit and units[u][1] == PACK - 1
+
         fetch(0, True)
         fetch(0, False)
         fetch(1, False)
-        for u in range(1, n_units + LAG + 1):
-            if u - 1 < n_units:
+        for u in range(1, last_unit + LAG + 2):
+            if u - 1 < last_unit:
                 add_pairs(u - 1)
-            if u < n_units:
+            if u <= last_unit:
                 fetch(u, True)
-            if 0 <= u - LAG - 1 and units[u - LAG - 1][1] == PACK - 1:
+            if closes_range(u - LAG - 1):
                 hand_on(units[u - LAG - 1][0])
-            if u - 1 < n_units:
+            if u - 1 <= last_unit:
                 root(u - 1)
-            if u + 1 < n_units:
+            if u + 1 <= last_unit:
                 fetch(u + 1, False)
-            if 0 <= u - LAG < n_units:
+            if 0 <= u - LAG <= last_unit:
                 finish(u - LAG)
-                if units[u - LAG][1] == PACK - 1:
-                    pack(units[u - LAG][0])
-        for i in range(4):
-            queue = nc.sync if i < 2 else nc.scalar
-            queue.dma_start(out_2[0][i:16:4, :].bitcast(I32), out_scales[i:P:32, :].bitcast(I32))
+            if closes_range(u - LAG):
+                pack(units[u - LAG][0])
+
+        for i in range(SCALE_ROWS):
+            queue = nc.sync if i < SCALE_ROWS // 2 else nc.scalar
+            queue.dma_start(
+                out_2[0][i:BLOCKS:SCALE_ROWS, :].bitcast(I32), out_scales[i:P:QUADRANT, :].bitcast(I32)
+            )

from contextlib import ExitStack

import concourse.mybir as mybir

K, T, S, H, C, W = 512, 2048, 512, 512, 512, 2048
FLOPS = 2 * K * H * S + 2 * H * C * S

F32 = mybir.dt.float32
BF16 = mybir.dt.bfloat16
I32 = mybir.dt.int32
U32 = mybir.dt.uint32
U16 = mybir.dt.uint16
U8 = mybir.dt.uint8
FP8X4 = mybir.dt.float8_e4m3fn_x4
FP4X4 = mybir.dt.float4_e2m1fn_x4
ACT = mybir.ActivationFunctionType
ALU = mybir.AluOpType

P = 128
PACK = 4
QUADRANT = 32
SCALE_ROWS = 4
BLOCKS = 16
PER_COLUMN = 16
HALF = S // 2
MEMBERS = W // S
PIECE = 256
FIRST_LOAD = 768
RANGES = ((0, 256), (256, 128), (384, 128))
VECTOR_FIRST, VECTOR_EVERY, VECTOR_LAST = 4, 4, 26
RING = 3
LAG = 3


def tile_picked_candehqgvar_none_po_kernel(
    tc, x_words, x_scales, w1_words, w1_scales, sl, th, gs, offs, n1, n2, cand, n3, out_0, out_1, out_2
):
    nc = tc.nc
    with ExitStack() as ctx:
        keep = ctx.enter_context(tc.tile_pool(name="keep", bufs=1))
        ring = ctx.enter_context(tc.tile_pool(name="ring", bufs=RING))
        psum = ctx.enter_context(tc.psum_pool(name="psum", bufs=1))

        def sbuf(name, shape, dtype):
            return keep.tile(shape, dtype, name=name, align_bytes=64)

        def load_list(name, src):
            tile = sbuf(name, list(src.shape), U16)
            nc.sync.dma_start(tile[:], src)
            return tile

        def load_per_row(name, src):
            tile = sbuf(name, [P, PACK], F32)
            nc.sync.dma_start(tile[:], src.rearrange("(p t) o -> p (t o)", t=PACK))
            return tile

        def half_cols(h):
            return slice(h * HALF, (h + 1) * HALF)

        def list_cols(first, count):
            return slice(first // PER_COLUMN, (first + count) // PER_COLUMN)

        def in_bank(banks, t, j0, width):
            return banks[t, j0 // HALF][:, j0 % HALF : j0 % HALF + width]

        x_scale_table = sbuf("x_scale_table", [P, T], U8)
        w_scale_raw = keep.tile([P, H], U8, name="w_scale_raw", tag="w_scale_raw", align_bytes=64)

        nc.vector.memset(x_scale_table[:].bitcast(I32), 0)
        warm_in = sbuf("warm_in", [P, 1], F32)
        warm_out = sbuf("warm_out", [P, 2], F32)
        nc.gpsimd.memset(warm_in[:], 0.0)
        nc.scalar.activation(warm_out[:, 0:1], warm_in[:], ACT.Sigmoid)

        offs_t = load_list("offs_t", offs)
        x_word_table = sbuf("x_word_table", [P, T], I32)
        x_word_rows = x_words[0].rearrange("p n t -> p (n t)").bitcast(I32)
        nc.sync.dma_start(x_word_table[:, :FIRST_LOAD], x_word_rows[:, :FIRST_LOAD])
        for i in range(SCALE_ROWS):
            nc.sync.dma_start(
                x_scale_table[i:P:QUADRANT, :].bitcast(I32), x_scales[0][i:BLOCKS:SCALE_ROWS, :].bitcast(I32)
            )
        nc.sync.dma_start(x_word_table[:, FIRST_LOAD:], x_word_rows[:, FIRST_LOAD:])
        w_word_raw = sbuf("w_word_raw", [P, 2 * H], U8)
        nc.sync.dma_start(w_word_raw[:].bitcast(I32), w1_words[0].bitcast(I32))
        for q in range(P // QUADRANT):
            rows = w1_scales[0][SCALE_ROWS * q : SCALE_ROWS * (q + 1), :].bitcast(I32)
            nc.sync.dma_start(
                w_scale_raw[QUADRANT * q : QUADRANT * (q + 1), :].bitcast(I32),
                rows.unsqueeze(0).broadcast_to([QUADRANT // SCALE_ROWS, SCALE_ROWS, rows.shape[1]]),
            )
        cand_t = load_list("cand_t", cand)
        n1_t = load_list("n1_t", n1)
        sl_t = load_per_row("sl_t", sl)
        th_t = load_per_row("th_t", th)
        n2_t = load_list("n2_t", n2)
        gs_t = load_per_row("gs_t", gs)
        n3_t = load_list("n3_t", n3)

        w_words = sbuf("w_words", [P, 2 * H], U8)
        w_scales = sbuf("w_scales", [P, H], U8)
        nc.scalar.copy(
            w_words[:].bitcast(U16).rearrange("p (t m) -> p t m", t=PACK),
            w_word_raw[:].bitcast(U16).rearrange("p (m t) -> p t m", t=PACK),
        )

        tok_scales = sbuf("tok_scales", [P, S], U8)
        nc.vector.tensor_copy(tok_scales[:], x_scale_table[:].indirect(offs_t[:]))
        tok_words = [sbuf(f"tok_words{h}", [P, HALF], U32) for h in range(2)]
        for h in range(2):
            nc.vector.tensor_copy(
                tok_words[h][:], x_word_table[:].bitcast(U32).indirect(offs_t[:, list_cols(h * HALF, HALF)])
            )

        w_scales_dealt = w_scales[:].rearrange("p (t m) -> p t m", t=PACK)
        w_scales_given = w_scale_raw[:].rearrange("p (m t) -> p t m", t=PACK)
        nc.vector.tensor_copy(w_scales_dealt[:, 0, :], w_scales_given[:, 0, :])
        nc.vector.tensor_copy(w_scales_dealt[:, 1:, :], w_scales_given[:, 1:, :])

        cand_words = keep.tile([P, C], U32, name="cand_words", tag="w_scale_raw", align_bytes=64)
        nc.vector.tensor_copy(
            cand_words[:].rearrange("p (t m) -> p m t", t=PACK), x_word_table[:].bitcast(U32).indirect(cand_t[:])
        )
        cand_scales = sbuf("cand_scales", [P, C], U8)
        nc.vector.tensor_copy(
            cand_scales[:].rearrange("p (t m) -> p m t", t=PACK), x_scale_table[:].indirect(cand_t[:])
        )

        gate_bias = sbuf("gate_bias", [P, PACK], F32)
        nc.vector.scalar_tensor_tensor(gate_bias[:], sl_t[:], -1.0, th_t[:], ALU.mult, ALU.mult)

        y_bank = {}
        for t in range(PACK):
            for h in range(2):
                y_bank[t, h] = psum.tile([P, HALF], F32, name=f"y_bank{t}{h}", tag=f"bank{t}{h}")
                nc.tensor.matmul_mx(
                    out=y_bank[t, h][:],
                    lhsT=w_words[:, 2 * P * t : 2 * P * (t + 1)].bitcast(FP4X4),
                    lhsT_scale=w_scales[:, P * t : P * (t + 1)],
                    rhs=tok_words[h][:].bitcast(FP8X4),
                    rhs_scale=tok_scales[:, half_cols(h)],
                    start=True,
                    stop=True,
                )

        minus_y = [sbuf(f"minus_y{t}", [P, S], F32) for t in range(PACK)]
        plus_y = [sbuf(f"plus_y{t}", [P, S], F32) for t in range(PACK)]
        st = [sbuf(f"st{t}", [P, S], F32) for t in range(PACK)]
        sg = [sbuf(f"sg{t}", [P, S], F32) for t in range(PACK)]
        z_rows = [sbuf(f"z_rows{r}", [P, PACK, width], BF16) for r, (j0, width) in enumerate(RANGES)]
        z_words = [sbuf(f"z_words{r}", [P, width], U32) for r, (j0, width) in enumerate(RANGES)]
        z_scales = [sbuf(f"z_scales{r}", [P, width], U8) for r, (j0, width) in enumerate(RANGES)]
        sq = [sbuf(f"sq{t}", [P, S], F32) for t in range(PACK)]
        s_bank = {}

        def leave_psum(t):
            for h in range(2):
                nc.scalar.activation(minus_y[t][:, half_cols(h)], y_bank[t, h][:], ACT.Copy, scale=-1.0)
                nc.scalar.activation(plus_y[t][:, half_cols(h)], y_bank[t, h][:], ACT.Copy)

        def difference(t):
            for h in range(2):
                nc.vector.tensor_tensor(
                    st[t][:, half_cols(h)],
                    minus_y[t][:].indirect(n1_t[:, list_cols(h * HALF, HALF)]),
                    plus_y[t][:, half_cols(h)],
                    ALU.add,
                )

        def gate(t, r):
            j0, width = RANGES[r]
            nc.scalar.activation(
                sg[t][:, j0 : j0 + width],
                st[t][:].indirect(n2_t[:, list_cols(j0, width)]),
                ACT.Sigmoid,
                bias=gate_bias[:, t : t + 1],
                scale=sl_t[:, t : t + 1],
            )

        def weigh(t, r):
            j0, width = RANGES[r]
            nc.vector.scalar_tensor_tensor(
                z_rows[r][:, t, :],
                in_bank(y_bank, t, j0, width),
                gs_t[:, t : t + 1],
                sg[t][:, j0 : j0 + width],
                ALU.mult,
                ALU.mult,
            )

        def interleave(packed, rows):
            nc.vector.tensor_copy(
                packed.rearrange("p (c i) t -> p c t i", i=4), rows.rearrange("p t (c i) -> p c t i", i=4)
            )

        def quantise_z(r):
            z_packed = keep.tile([P, RANGES[r][1], PACK], BF16, name=f"z_packed{r}", tag="z_packed", align_bytes=64)
            interleave(z_packed[:], z_rows[r][:])
            nc.vector.quantize_mx(
                out=z_words[r][:].bitcast(FP8X4), scales=z_scales[r][:], in_=z_packed[:].rearrange("p c t -> p (c t)")
            )

        def score(r):
            j0, width = RANGES[r]
            h = j0 // HALF
            for t in range(PACK):
                if (t, h) not in s_bank:
                    s_bank[t, h] = psum.tile([P, HALF], F32, name=f"s_bank{t}{h}", tag=f"bank{t}{h}")
                nc.tensor.matmul_mx(
                    out=in_bank(s_bank, t, j0, width),
                    lhsT=cand_words[:, P * t : P * (t + 1)].bitcast(FP8X4),
                    lhsT_scale=cand_scales[:, P * t : P * (t + 1)],
                    rhs=z_words[r][:].bitcast(FP8X4),
                    rhs_scale=z_scales[r][:],
                    start=True,
                    stop=True,
                )
                if (j0 + width) % HALF == 0:
                    nc.scalar.activation(sq[t][:, half_cols(h)], s_bank[t, h][:], ACT.Square, scale=0.0625)

        leave_psum(0)
        for t in range(PACK):
            if t + 1 < PACK:
                leave_psum(t + 1)
            difference(t)
        for r in range(len(RANGES)):
            for t in range(PACK):
                gate(t, r)
        nc.scalar.activation(warm_out[:, 1:2], sg[PACK - 1][:, S - 1 : S], ACT.Abs_reciprocal_sqrt, bias=0.5)
        for r in range(len(RANGES)):
            for t in range(PACK):
                weigh(t, r)
            quantise_z(r)
            if r == 0:
                score(r)
        for r in range(1, len(RANGES)):
            score(r)

        out_words = sbuf("out_words", [P, S], U32)
        out_scales = sbuf("out_scales", [P, S], U8)
        out_rows = out_0.rearrange("(p t) j -> p t j", t=PACK)
        out_word_rows = out_1[0].rearrange("p n t -> p (n t)").bitcast(I32)

        units = [(r, t) for r in range(len(RANGES)) for t in range(PACK)]
        last_unit = len(units) - 1
        result = [sbuf(f"result{r}", [P, PACK, width], F32) for r, (j0, width) in enumerate(RANGES)]
        members, pairs, inv_root, out_packed = {}, {}, {}, {}

        def fetch(u, on_vector):
            r, t = units[u]
            j0, width = RANGES[r]
            if u not in members:
                members[u] = ring.tile([P, width * MEMBERS], F32, name=f"members{u}", tag="members")
            first_piece = (j0 * PACK + t * width) * MEMBERS // PIECE
            for k in range(width * MEMBERS // PIECE):
                looked_up = sq[t][:].indirect(n3_t[:, list_cols(j0 * MEMBERS + k * PIECE, PIECE)])
                dst = members[u][:, k * PIECE : (k + 1) * PIECE]
                piece = first_piece + k
                for_vector = piece < VECTOR_FIRST or (piece % VECTOR_EVERY == 1 and piece <= VECTOR_LAST)
                if for_vector and on_vector:
                    nc.vector.tensor_copy(dst, looked_up)
                if not for_vector and not on_vector:
                    nc.scalar.activation(dst, looked_up, ACT.Copy)

        def by_column(u):
            return members[u][:].rearrange("p (j m) -> p j m", m=MEMBERS)

        def add_pairs(u):
            pairs[u] = sbuf(f"pairs{u}", [P, RANGES[units[u][0]][1], 2], F32)
            nc.vector.tensor_tensor(pairs[u][:], by_column(u)[:, :, 0:2], by_column(u)[:, :, 2:4], ALU.add)

        def root(u):
            width = RANGES[units[u][0]][1]
            qs = sbuf(f"qs{u}", [P, width], F32)
            if u == last_unit:
                nc.vector.tensor_reduce(qs[:], by_column(u), mybir.AxisListType.X, ALU.add)
            else:
                nc.vector.tensor_tensor(qs[:], pairs[u][:, :, 0], pairs[u][:, :, 1], ALU.add)
            inv_root[u] = sbuf(f"inv_root{u}", [P, width], F32)
            nc.scalar.activation(inv_root[u][:], qs[:], ACT.Abs_reciprocal_sqrt, bias=0.5)

        def finish(u):
            r, t = units[u]
            j0, width = RANGES[r]
            nc.vector.scalar_tensor_tensor(
                result[r][:, t, :], in_bank(s_bank, t, j0, width), 0.0625, inv_root[u][:], ALU.mult, ALU.mult
            )
            nc.sync.dma_start(out_rows[:, t, j0 : j0 + width], result[r][:, t, :])

        def pack(r):
            out_packed[r] = sbuf(f"out_packed{r}", [P, RANGES[r][1], PACK], BF16)
            interleave(out_packed[r][:], result[r][:])

        def hand_on(r):
            j0, width = RANGES[r]
            js = slice(j0, j0 + width)
            nc.vector.quantize_mx(
                out=out_words[:, js].bitcast(FP8X4),
                scales=out_scales[:, js],
                in_=out_packed[r][:].rearrange("p c t -> p (c t)"),
            )
            nc.sync.dma_start(out_word_rows[:, js], out_words[:, js].bitcast(I32))

        def closes_range(u):
            return 0 <= u <= last_unit and units[u][1] == PACK - 1

        fetch(0, True)
        fetch(0, False)
        fetch(1, False)
        for u in range(1, last_unit + LAG + 2):
            if u - 1 < last_unit:
                add_pairs(u - 1)
            if u <= last_unit:
                fetch(u, True)
            if closes_range(u - LAG - 1):
                hand_on(units[u - LAG - 1][0])
            if u - 1 <= last_unit:
                root(u - 1)
            if u + 1 <= last_unit:
                fetch(u + 1, False)
            if 0 <= u - LAG <= last_unit:
                finish(u - LAG)
            if closes_range(u - LAG):
                pack(units[u - LAG][0])

        for i in range(SCALE_ROWS):
            queue = nc.sync if i < SCALE_ROWS // 2 else nc.scalar
            queue.dma_start(
                out_2[0][i:BLOCKS:SCALE_ROWS, :].bitcast(I32), out_scales[i:P:QUADRANT, :].bitcast(I32)
            )
